import numpy as np
import ml_dtypes


def mxq(x, axis, fmt="e4m3"):
    dtype, down = {"e4m3": (ml_dtypes.float8_e4m3fn, 7), "e5m2": (ml_dtypes.float8_e5m2, 14)}[fmt]
    v = np.moveaxis(np.asarray(x, np.float32).astype(ml_dtypes.bfloat16).astype(np.float64), axis, -1)
    blocks = v.reshape(v.shape[:-1] + (-1, 32))
    amax = np.abs(blocks).max(-1, keepdims=True)
    byte = np.maximum(np.where(amax > 0, np.frexp(amax)[1] - 1 + 127, 0) - down, 1)
    scale = np.exp2(byte - 127.0)
    codes = (blocks / scale).astype(np.float32).astype(dtype).astype(np.float64)
    return np.moveaxis((codes * scale).reshape(v.shape), -1, axis)


WIDE = False


def mx_kscale(k):
    if not WIDE:
        return np.ones(k)
    levels = np.array([10, -10, 5, -5, 0])
    if k % 512:
        return np.exp2(np.random.permutation(np.resize(levels, k // 32))).repeat(32)
    a = np.empty((k // 512, 16))
    for p in range(k // 512):
        a[p, :8] = np.random.permutation(np.resize(levels, 8))
        for g in range(8):
            far = levels[np.abs(levels - a[p, g]) >= 10]
            a[p, g + 8] = far[np.random.randint(len(far))]
    return np.exp2(a.ravel()).repeat(32)


def f64(x):
    return np.asarray(x).astype(np.float64)


def striped8(idx):
    return np.asarray(idx).reshape(8, -1, 16).transpose(0, 2, 1).reshape(128, -1).astype(np.uint16)


def unstriped8(offs):
    return offs.reshape(8, 16, -1).transpose(0, 2, 1).reshape(8, -1).astype(np.int64)


def pick8(x, idx, run):
    r = np.arange(len(x))
    return x[r[:, None], idx[r % (8 * run) // run]]


E2M1 = np.array([0.0, 0.5, 1.0, 1.5, 2.0, 3.0, 4.0, 6.0, -0.0, -0.5, -1.0, -1.5, -2.0, -3.0, -4.0, -6.0])


def pack_weight(w, fmt):
    k, n = w.shape
    w = f64(np.asarray(w, np.float32).astype(ml_dtypes.bfloat16)).reshape(k // 32, 32, n)
    amax = np.abs(w).max(1)
    if fmt == "e4m3":
        byte = np.frexp(amax)[1] - 1 + 127 - 7
    else:
        mant, ex = np.frexp(amax / 6.0)
        byte = np.where(mant > 0.5, ex, ex - 1) + 127
    byte = np.clip(np.where(amax > 0, byte, 1), 1, 254)
    scaled = (w * np.exp2(127.0 - byte)[:, None, :]).reshape(k, n).astype(np.float32)
    by_word = np.ascontiguousarray(scaled.reshape(k // 512, 128, 4, n).transpose(0, 1, 3, 2))
    if fmt == "e4m3":
        words = by_word.astype(ml_dtypes.float8_e4m3fn).view(np.uint8)
    else:
        c = by_word.astype(ml_dtypes.float4_e2m1fn).view(np.uint8) & 0xF
        words = (c[..., 0::2] | (c[..., 1::2] << 4)).reshape(k // 512, 128, 2 * n)
    return np.ascontiguousarray(words), np.ascontiguousarray(byte.astype(np.uint8).reshape(k // 512, 16, n))


def unpack_weight(words, scales, fmt):
    g, _, n = scales.shape
    words = np.ascontiguousarray(words).reshape(g, 128, n, -1)
    if fmt == "e4m3":
        vals = words.view(ml_dtypes.float8_e4m3fn).astype(np.float64)
    else:
        nib = np.empty((g, 128, n, 4), np.uint8)
        nib[..., 0::2] = words & 0xF
        nib[..., 1::2] = words >> 4
        vals = E2M1[nib]
    vals = vals * np.repeat(np.exp2(scales.astype(np.float64) - 127.0), 8, axis=1)[..., None]
    return vals.transpose(0, 1, 3, 2).reshape(g * 512, n)


D, T, Q, I, E = 512, 1024, 128, 512, 512


def setup_inputs():
    n = np.random.standard_normal
    idx = np.stack([np.random.permutation(T)[:I] for _ in range(8)])
    idx2 = np.stack([np.random.permutation(T)[:I] for _ in range(8)])
    fd = mx_kscale(D)
    ft = mx_kscale(T)
    keysp = pack_weight(n((D, T)) / fd[:, None], "e4m3")
    return {
        "query": (n((D, Q)) * 0.6 / np.sqrt(D) * fd[:, None]).astype(np.float32),
        "keys_words": keysp[0],
        "keys_scales": keysp[1],
        "share": (np.random.uniform(0.4, 1.0, (Q, 1))).astype(np.float32),
        "fac": (np.random.uniform(8.0, 32.0, (1, T)) * ft).astype(np.float32),
        "vals": (n((T, E)) / ft[:, None]).astype(np.float32),
        "offs": striped8(idx),
        "offs2": striped8(idx2),
    }


def reference(query, keys_words, keys_scales, share, fac, vals, offs, offs2):
    idx = unstriped8(offs)
    idx2 = unstriped8(offs2)
    keysu = unpack_weight(keys_words, keys_scales, "e4m3")
    queryq = mxq(f64(query), 0, "e4m3")
    a = queryq.T @ keysu
    dl = (pick8(a, idx2, 16) - pick8(a, idx, 16)) * f64(share)
    df = np.zeros((Q, T))
    df[np.arange(Q)[:, None], idx[np.arange(Q) % 128 // 16]] = dl
    s = a + df
    p = np.exp(s - np.max(s, axis=1, keepdims=True))
    w = p * f64(fac) / np.sum(p, axis=1, keepdims=True)
    wt = w.T
    wtq = mxq(wt, 0, "e4m3")
    valsq = mxq(f64(vals), 0, "e4m3")
    o = wtq.T @ valsq
    return o

@@ -1,0 +1,191 @@
+from contextlib import ExitStack
+
+import concourse.mybir as mybir
+from concourse.masks import make_identity
+
+D, T, Q, SLOTS, E = 512, 1024, 128, 512, 512
+FLOPS = 2 * D * Q * T + 2 * T * Q * E
+
+F32 = mybir.dt.float32
+BF16 = mybir.dt.bfloat16
+I32 = mybir.dt.int32
+U32 = mybir.dt.uint32
+U16 = mybir.dt.uint16
+U8 = mybir.dt.uint8
+FP8X4 = mybir.dt.float8_e4m3fn_x4
+ALU = mybir.AluOpType
+ACT = mybir.ActivationFunctionType
+
+P = 128
+PACK = 4
+K_PASS = P * PACK
+PASSES = T // K_PASS
+E_HALF = E // 2
+
+
+def tile_attend_swapscores_heads_kernel(tc, query, keys_words, keys_scales, share, fac, vals, offs, offs2, out):
+    nc = tc.nc
+    with ExitStack() as ctx:
+        lists = ctx.enter_context(tc.tile_pool(name="lists", bufs=1))
+        sb = ctx.enter_context(tc.tile_pool(name="sb", bufs=1))
+        ps = ctx.enter_context(tc.psum_pool(name="ps", bufs=1))
+
+        k_scales = sb.tile([P, T], U8, name="k_scales", align_bytes=64)
+        nc.vector.memset(k_scales[:].bitcast(I32), 0)
+        q_raw = sb.tile([P, PACK, Q], F32, name="q_raw")
+        nc.sync.dma_start(out=q_raw[:], in_=query.rearrange("(p j) q -> p j q", j=PACK))
+        for quad in range(4):
+            nc.scalar.dma_start(
+                out=k_scales[32 * quad : 32 * quad + 4, :].bitcast(I32),
+                in_=keys_scales[0, 4 * quad : 4 * quad + 4, :].bitcast(I32),
+            )
+        key_rows = keys_words[0].rearrange("p n t -> p (n t)")
+        k_words = []
+        for h in range(2):
+            kw = sb.tile([P, K_PASS], U32, name=f"k_words{h}", tag=f"k_words{h}", align_bytes=64)
+            nc.sync.dma_start(out=kw[:].bitcast(I32), in_=key_rows[:, h * 2048 : (h + 1) * 2048].bitcast(I32))
+            k_words.append(kw)
+        second = lists.tile([P, SLOTS // 16], U16, name="second")
+        nc.sync.dma_start(second[:], offs2)
+        first = lists.tile([P, SLOTS // 16], U16, name="first")
+        nc.sync.dma_start(first[:], offs)
+        share_col = sb.tile([P, 1], F32, name="share_col")
+        nc.sync.dma_start(out=share_col[:], in_=share)
+        v_raw = []
+        for g in range(PASSES):
+            vr = sb.tile([P, PACK, E], F32, name=f"v_raw{g}", tag=f"v_raw{g}")
+            nc.sync.dma_start(out=vr[:], in_=vals[g * K_PASS : (g + 1) * K_PASS, :].rearrange("(p j) e -> p j e", j=PACK))
+            v_raw.append(vr)
+        fac_cols = sb.tile([P, PASSES, PACK], F32, name="fac_cols")
+        nc.sync.dma_start(out=fac_cols[:], in_=fac[0].rearrange("(g p j) -> p g j", g=PASSES, j=PACK))
+
+        ident = sb.tile([P, P], F32, name="ident")
+        make_identity(nc, ident[:])
+        df = sb.tile([P, T], F32, name="df")
+        nc.gpsimd.memset(df[:], 0.0)
+
+        q_bf = sb.tile([P, Q, PACK], BF16, name="q_bf", align_bytes=64)
+        nc.vector.tensor_copy(
+            out=q_bf[:].rearrange("p (c i) j -> p c j i", i=4),
+            in_=q_raw[:].rearrange("p j (c i) -> p c j i", i=4),
+        )
+        q_codes = sb.tile([P, Q], U32, name="q_codes", align_bytes=64)
+        q_scales = sb.tile([P, Q], U8, name="q_scales", align_bytes=64)
+        nc.vector.quantize_mx(out=q_codes[:].bitcast(FP8X4), scales=q_scales[:], in_=q_bf[:].rearrange("p q j -> p (q j)"))
+
+        a_sb = sb.tile([P, T], F32, name="a_sb")
+        a_ps = []
+        for c in range(4):
+            cols = slice(c * 256, (c + 1) * 256)
+            bank = ps.tile([P, 256], F32, name=f"a_ps{c}", tag=f"bank{c}")
+            nc.tensor.matmul_mx(
+                out=bank[:],
+                lhsT=q_codes[:].bitcast(FP8X4),
+                lhsT_scale=q_scales[:],
+                rhs=k_words[c // 2][:, (c % 2) * 256 : (c % 2 + 1) * 256].bitcast(FP8X4),
+                rhs_scale=k_scales[:, cols],
+                start=True,
+                stop=True,
+            )
+            if c % 2 == 0:
+                nc.scalar.copy(out=a_sb[:, cols], in_=bank[:])
+            else:
+                nc.vector.tensor_copy(out=a_sb[:, cols], in_=bank[:])
+            a_ps.append(bank)
+
+        share_wide = sb.tile([P, SLOTS], F32, name="share_wide", tag="k_words1", align_bytes=64)
+        nc.scalar.copy(out=share_wide[:], in_=share_col[:].to_broadcast([P, SLOTS]))
+
+        fac_ps = []
+        for g in range(PASSES):
+            bank = ps.tile([P, PACK, P], F32, name=f"fac_ps{g}")
+            for j in range(PACK):
+                nc.tensor.transpose(bank[:, j, :], fac_cols[:, g, j : j + 1].to_broadcast([P, P]), ident[:])
+            fac_ps.append(bank)
+
+        own = sb.tile([P, SLOTS], F32, name="own")
+        diff = sb.tile([P, SLOTS], F32, name="diff")
+        for h in range(2):
+            nc.vector.tensor_copy(own[:, h * 256 : (h + 1) * 256], a_sb[:].indirect(first[:, h * 16 : (h + 1) * 16]))
+        for h in range(2):
+            nc.vector.tensor_tensor(
+                diff[:, h * 256 : (h + 1) * 256],
+                a_sb[:].indirect(second[:, h * 16 : (h + 1) * 16]),
+                own[:, h * 256 : (h + 1) * 256],
+                ALU.subtract,
+            )
+        nc.vector.tensor_tensor(df[:].indirect(first[:]), diff[:], share_wide[:], ALU.mult)
+
+        v_bf = []
+        for g in range(PASSES):
+            vb = sb.tile([P, E, PACK], BF16, name=f"v_bf{g}", align_bytes=64)
+            nc.scalar.copy(
+                out=vb[:].rearrange("p (c i) j -> p c j i", i=4),
+                in_=v_raw[g][:].rearrange("p j (c i) -> p c j i", i=4),
+            )
+            v_bf.append(vb)
+
+        s = sb.tile([P, T], F32, name="s", tag="s", align_bytes=64)
+        nc.vector.tensor_tensor(s[:], a_sb[:], df[:], ALU.add)
+        neg_s = sb.tile([P, T], F32, name="neg_s")
+        neg_max = sb.tile([P, 1], F32, name="neg_max")
+        nc.vector.tensor_scalar(neg_s[:], s[:], -1.0, None, ALU.mult, ALU.min, accum_out=neg_max[:])
+        p = sb.tile([P, T], F32, name="p", tag="v_raw1")
+        row_sum = sb.tile([P, 1], F32, name="row_sum")
+        nc.scalar.activation(p[:], neg_s[:], ACT.Exp, bias=neg_max[:], scale=-1.0, accum_out=row_sum[:])
+
+        v_codes = sb.tile([P, PASSES, E], U32, name="v_codes", tag="s", align_bytes=64)
+        v_scales = sb.tile([P, PASSES, E], U8, name="v_scales", align_bytes=64)
+        for g in range(PASSES):
+            nc.vector.quantize_mx(
+                out=v_codes[:, g, :].bitcast(FP8X4), scales=v_scales[:, g, :], in_=v_bf[g][:].rearrange("p e j -> p (e j)")
+            )
+
+        inv_sum = sb.tile([P, 1], F32, name="inv_sum")
+        nc.vector.reciprocal(inv_sum[:], row_sum[:])
+
+        o_ps = [ps.tile([P, E_HALF], F32, name=f"o_ps{c}", tag=f"bank{c}") for c in range(2)]
+        w_bf = []
+        for g in range(PASSES):
+            wb = sb.tile([P, P, PACK], BF16, name=f"w_bf{g}")
+            nc.vector.scalar_tensor_tensor(
+                wb[:],
+                p[:, g * K_PASS : (g + 1) * K_PASS].rearrange("q (r j) -> q r j", j=PACK),
+                inv_sum[:],
+                fac_ps[g][:].rearrange("q j r -> q r j"),
+                ALU.mult,
+                ALU.mult,
+            )
+            w_bf.append(wb)
+        for g in range(PASSES):
+            pairs = w_bf[g][:].rearrange("q r j -> q (r j)").bitcast(F32)
+            turned = ps.tile([P, 2, Q], F32, name=f"turned{g}", tag=f"bank{2 + g}")
+            for u in range(2):
+                nc.tensor.transpose(turned[:, u, :], pairs[:, u : 2 * P : 2], ident[:])
+            wt_bf = sb.tile([P, Q * PACK], BF16, name=f"wt_bf{g}", align_bytes=64)
+            nc.scalar.copy(
+                out=wt_bf[:].bitcast(F32).rearrange("r (q u) -> r q u", u=2), in_=turned[:].rearrange("r u q -> r q u")
+            )
+            wt_codes = sb.tile([P, Q], U32, name=f"wt_codes{g}", align_bytes=64)
+            wt_scales = sb.tile([P, Q], U8, name=f"wt_scales{g}", align_bytes=64)
+            nc.vector.quantize_mx(out=wt_codes[:].bitcast(FP8X4), scales=wt_scales[:], in_=wt_bf[:])
+            for c in range(2):
+                cols = slice(c * E_HALF, (c + 1) * E_HALF)
+                nc.tensor.matmul_mx(
+                    out=o_ps[c][:],
+                    lhsT=wt_codes[:].bitcast(FP8X4),
+                    lhsT_scale=wt_scales[:],
+                    rhs=v_codes[:, g, cols].bitcast(FP8X4),
+                    rhs_scale=v_scales[:, g, cols],
+                    start=(g == 0),
+                    stop=(g == PASSES - 1),
+                )
+        for c in range(2):
+            cols = slice(c * E_HALF, (c + 1) * E_HALF)
+            res = sb.tile([P, E_HALF], F32, name=f"res{c}")
+            if c == 0:
+                nc.scalar.copy(out=res[:], in_=o_ps[c][:])
+                nc.scalar.dma_start(out=out[:, cols], in_=res[:])
+            else:
+                nc.vector.tensor_copy(out=res[:], in_=o_ps[c][:])
+                nc.sync.dma_start(out=out[:, cols], in_=res[:])

@@ -62,16 +62,23 @@ def tile_attend_swapscores_heads_kernel(tc, query, keys_words, keys_scales, shar
         ident = sb.tile([P, P], F32, name="ident")
         make_identity(nc, ident[:])
         df = sb.tile([P, T], F32, name="df")
-        nc.gpsimd.memset(df[:], 0.0)
+        nc.vector.memset(df[:], 0.0)
 
-        q_bf = sb.tile([P, Q, PACK], BF16, name="q_bf", align_bytes=64)
-        nc.vector.tensor_copy(
-            out=q_bf[:].rearrange("p (c i) j -> p c j i", i=4),
-            in_=q_raw[:].rearrange("p j (c i) -> p c j i", i=4),
-        )
         q_codes = sb.tile([P, Q], U32, name="q_codes", align_bytes=64)
         q_scales = sb.tile([P, Q], U8, name="q_scales", align_bytes=64)
-        nc.vector.quantize_mx(out=q_codes[:].bitcast(FP8X4), scales=q_scales[:], in_=q_bf[:].rearrange("p q j -> p (q j)"))
+        q_bf = []
+        for h in range(2):
+            qb = sb.tile([P, 64, PACK], BF16, name=f"q_bf{h}", align_bytes=64)
+            nc.vector.tensor_copy(
+                out=qb[:].rearrange("p (c i) j -> p c j i", i=4),
+                in_=q_raw[:, :, h * 64 : (h + 1) * 64].rearrange("p j (c i) -> p c j i", i=4),
+            )
+            q_bf.append(qb)
+        for h in range(2):
+            cols = slice(h * 64, (h + 1) * 64)
+            nc.vector.quantize_mx(
+                out=q_codes[:, cols].bitcast(FP8X4), scales=q_scales[:, cols], in_=q_bf[h][:].rearrange("p q j -> p (q j)")
+            )
 
         a_sb = sb.tile([P, T], F32, name="a_sb")
         a_ps = []
@@ -87,7 +94,7 @@ def tile_attend_swapscores_heads_kernel(tc, query, keys_words, keys_scales, shar
                 start=True,
                 stop=True,
             )
-            if c % 2 == 0:
+            if c % 2 == 1:
                 nc.scalar.copy(out=a_sb[:, cols], in_=bank[:])
             else:
                 nc.vector.tensor_copy(out=a_sb[:, cols], in_=bank[:])
@@ -145,23 +152,20 @@ def tile_attend_swapscores_heads_kernel(tc, query, keys_words, keys_scales, shar
         nc.vector.reciprocal(inv_sum[:], row_sum[:])
 
         o_ps = [ps.tile([P, E_HALF], F32, name=f"o_ps{c}", tag=f"bank{c}") for c in range(2)]
-        w_bf = []
+        turned_banks = []
         for g in range(PASSES):
-            wb = sb.tile([P, P, PACK], BF16, name=f"w_bf{g}")
-            nc.vector.scalar_tensor_tensor(
-                wb[:],
-                p[:, g * K_PASS : (g + 1) * K_PASS].rearrange("q (r j) -> q r j", j=PACK),
-                inv_sum[:],
-                fac_ps[g][:].rearrange("q j r -> q r j"),
-                ALU.mult,
-                ALU.mult,
-            )
-            w_bf.append(wb)
-        for g in range(PASSES):
-            pairs = w_bf[g][:].rearrange("q r j -> q (r j)").bitcast(F32)
+            p_pass = p[:, g * K_PASS : (g + 1) * K_PASS].rearrange("q (r j) -> q r j", j=PACK)
+            fac_pass = fac_ps[g][:].rearrange("q j r -> q r j")
             turned = ps.tile([P, 2, Q], F32, name=f"turned{g}", tag=f"bank{2 + g}")
             for u in range(2):
-                nc.tensor.transpose(turned[:, u, :], pairs[:, u : 2 * P : 2], ident[:])
+                wb = sb.tile([P, P, 2], BF16, name=f"w_bf{g}{u}")
+                nc.vector.scalar_tensor_tensor(
+                    wb[:], p_pass[:, :, 2 * u : 2 * u + 2], inv_sum[:], fac_pass[:, :, 2 * u : 2 * u + 2], ALU.mult, ALU.mult
+                )
+                nc.tensor.transpose(turned[:, u, :], wb[:].rearrange("q r e -> q (r e)").bitcast(F32), ident[:])
+            turned_banks.append(turned)
+        for g in range(PASSES):
+            turned = turned_banks[g]
             wt_bf = sb.tile([P, Q * PACK], BF16, name=f"wt_bf{g}", align_bytes=64)
             nc.scalar.copy(
                 out=wt_bf[:].bitcast(F32).rearrange("r (q u) -> r q u", u=2), in_=turned[:].rearrange("r u q -> r q u")

@@ -20,7 +20,7 @@ P = 128
 PACK = 4
 K_PASS = P * PACK
 PASSES = T // K_PASS
-E_HALF = E // 2
+E_HALF = E // 4
 
 
 def tile_attend_swapscores_heads_kernel(tc, query, keys_words, keys_scales, share, fac, vals, offs, offs2, out):
@@ -133,10 +133,15 @@ def tile_attend_swapscores_heads_kernel(tc, query, keys_words, keys_scales, shar
             v_bf.append(vb)
 
         s = sb.tile([P, T], F32, name="s", tag="s", align_bytes=64)
-        nc.vector.tensor_tensor(s[:], a_sb[:], df[:], ALU.add)
+        nc.gpsimd.tensor_tensor(s[:, 512:], a_sb[:, 512:], df[:, 512:], ALU.add)
+        for c in range(2):
+            cols = slice(c * 256, (c + 1) * 256)
+            nc.vector.tensor_tensor(s[:, cols], a_ps[c][:], df[:, cols], ALU.add)
         neg_s = sb.tile([P, T], F32, name="neg_s")
         neg_max = sb.tile([P, 1], F32, name="neg_max")
-        nc.vector.tensor_scalar(neg_s[:], s[:], -1.0, None, ALU.mult, ALU.min, accum_out=neg_max[:])
+        neg_max_head = sb.tile([P, 1], F32, name="neg_max_head")
+        nc.vector.tensor_scalar(neg_s[:, :256], s[:, :256], -1.0, None, ALU.mult, ALU.min, accum_out=neg_max_head[:])
+        nc.vector.tensor_scalar(neg_s[:, 256:], s[:, 256:], -1.0, neg_max_head[:], ALU.mult, ALU.min, accum_out=neg_max[:])
         p = sb.tile([P, T], F32, name="p", tag="v_raw1")
         row_sum = sb.tile([P, 1], F32, name="row_sum")
         nc.scalar.activation(p[:], neg_s[:], ACT.Exp, bias=neg_max[:], scale=-1.0, accum_out=row_sum[:])
@@ -151,12 +156,12 @@ def tile_attend_swapscores_heads_kernel(tc, query, keys_words, keys_scales, shar
         inv_sum = sb.tile([P, 1], F32, name="inv_sum")
         nc.vector.reciprocal(inv_sum[:], row_sum[:])
 
-        o_ps = [ps.tile([P, E_HALF], F32, name=f"o_ps{c}", tag=f"bank{c}") for c in range(2)]
+        o_ps = [ps.tile([P, E_HALF], F32, name=f"o_ps{c}", tag=f"bank{c}") for c in range(4)]
         turned_banks = []
         for g in range(PASSES):
             p_pass = p[:, g * K_PASS : (g + 1) * K_PASS].rearrange("q (r j) -> q r j", j=PACK)
             fac_pass = fac_ps[g][:].rearrange("q j r -> q r j")
-            turned = ps.tile([P, 2, Q], F32, name=f"turned{g}", tag=f"bank{2 + g}")
+            turned = ps.tile([P, 2, Q], F32, name=f"turned{g}", tag=f"bank{4 + g}")
             for u in range(2):
                 wb = sb.tile([P, P, 2], BF16, name=f"w_bf{g}{u}")
                 nc.vector.scalar_tensor_tensor(
@@ -173,7 +178,7 @@ def tile_attend_swapscores_heads_kernel(tc, query, keys_words, keys_scales, shar
             wt_codes = sb.tile([P, Q], U32, name=f"wt_codes{g}", align_bytes=64)
             wt_scales = sb.tile([P, Q], U8, name=f"wt_scales{g}", align_bytes=64)
             nc.vector.quantize_mx(out=wt_codes[:].bitcast(FP8X4), scales=wt_scales[:], in_=wt_bf[:])
-            for c in range(2):
+            for c in range(4):
                 cols = slice(c * E_HALF, (c + 1) * E_HALF)
                 nc.tensor.matmul_mx(
                     out=o_ps[c][:],
@@ -184,12 +189,11 @@ def tile_attend_swapscores_heads_kernel(tc, query, keys_words, keys_scales, shar
                     start=(g == 0),
                     stop=(g == PASSES - 1),
                 )
-        for c in range(2):
+        for c in range(4):
             cols = slice(c * E_HALF, (c + 1) * E_HALF)
             res = sb.tile([P, E_HALF], F32, name=f"res{c}")
-            if c == 0:
+            if c % 2 == 0:
                 nc.scalar.copy(out=res[:], in_=o_ps[c][:])
-                nc.scalar.dma_start(out=out[:, cols], in_=res[:])
             else:
                 nc.vector.tensor_copy(out=res[:], in_=o_ps[c][:])
-                nc.sync.dma_start(out=out[:, cols], in_=res[:])
+            nc.sync.dma_start(out=out[:, cols], in_=res[:])

@@ -31,18 +31,18 @@ def tile_attend_swapscores_heads_kernel(tc, query, keys_words, keys_scales, shar
         ps = ctx.enter_context(tc.psum_pool(name="ps", bufs=1))
 
         k_scales = sb.tile([P, T], U8, name="k_scales", align_bytes=64)
-        nc.vector.memset(k_scales[:].bitcast(I32), 0)
+        nc.gpsimd.memset(k_scales[:].bitcast(I32), 0)
         q_raw = sb.tile([P, PACK, Q], F32, name="q_raw")
         nc.sync.dma_start(out=q_raw[:], in_=query.rearrange("(p j) q -> p j q", j=PACK))
         for quad in range(4):
-            nc.scalar.dma_start(
+            nc.sync.dma_start(
                 out=k_scales[32 * quad : 32 * quad + 4, :].bitcast(I32),
                 in_=keys_scales[0, 4 * quad : 4 * quad + 4, :].bitcast(I32),
             )
         key_rows = keys_words[0].rearrange("p n t -> p (n t)")
         k_words = []
         for h in range(2):
-            kw = sb.tile([P, K_PASS], U32, name=f"k_words{h}", tag=f"k_words{h}", align_bytes=64)
+            kw = sb.tile([P, K_PASS], U32, name=f"k_words{h}", align_bytes=64)
             nc.sync.dma_start(out=kw[:].bitcast(I32), in_=key_rows[:, h * 2048 : (h + 1) * 2048].bitcast(I32))
             k_words.append(kw)
         second = lists.tile([P, SLOTS // 16], U16, name="second")
@@ -50,7 +50,7 @@ def tile_attend_swapscores_heads_kernel(tc, query, keys_words, keys_scales, shar
         first = lists.tile([P, SLOTS // 16], U16, name="first")
         nc.sync.dma_start(first[:], offs)
         share_col = sb.tile([P, 1], F32, name="share_col")
-        nc.sync.dma_start(out=share_col[:], in_=share)
+        nc.scalar.dma_start(out=share_col[:], in_=share)
         v_raw = []
         for g in range(PASSES):
             vr = sb.tile([P, PACK, E], F32, name=f"v_raw{g}", tag=f"v_raw{g}")
@@ -100,7 +100,7 @@ def tile_attend_swapscores_heads_kernel(tc, query, keys_words, keys_scales, shar
                 nc.vector.tensor_copy(out=a_sb[:, cols], in_=bank[:])
             a_ps.append(bank)
 
-        share_wide = sb.tile([P, SLOTS], F32, name="share_wide", tag="k_words1", align_bytes=64)
+        share_wide = sb.tile([P, SLOTS], F32, name="share_wide")
         nc.scalar.copy(out=share_wide[:], in_=share_col[:].to_broadcast([P, SLOTS]))
 
         fac_ps = []

from contextlib import ExitStack

import concourse.mybir as mybir
from concourse.masks import make_identity

D, T, Q, SLOTS, E = 512, 1024, 128, 512, 512
FLOPS = 2 * D * Q * T + 2 * T * Q * E

F32 = mybir.dt.float32
BF16 = mybir.dt.bfloat16
I32 = mybir.dt.int32
U32 = mybir.dt.uint32
U16 = mybir.dt.uint16
U8 = mybir.dt.uint8
FP8X4 = mybir.dt.float8_e4m3fn_x4
ALU = mybir.AluOpType
ACT = mybir.ActivationFunctionType

P = 128
PACK = 4
K_PASS = P * PACK
PASSES = T // K_PASS
E_HALF = E // 4


def tile_attend_swapscores_heads_kernel(tc, query, keys_words, keys_scales, share, fac, vals, offs, offs2, out):
    nc = tc.nc
    with ExitStack() as ctx:
        lists = ctx.enter_context(tc.tile_pool(name="lists", bufs=1))
        sb = ctx.enter_context(tc.tile_pool(name="sb", bufs=1))
        ps = ctx.enter_context(tc.psum_pool(name="ps", bufs=1))

        k_scales = sb.tile([P, T], U8, name="k_scales", align_bytes=64)
        nc.gpsimd.memset(k_scales[:].bitcast(I32), 0)
        q_raw = sb.tile([P, PACK, Q], F32, name="q_raw")
        nc.sync.dma_start(out=q_raw[:], in_=query.rearrange("(p j) q -> p j q", j=PACK))
        for quad in range(4):
            nc.sync.dma_start(
                out=k_scales[32 * quad : 32 * quad + 4, :].bitcast(I32),
                in_=keys_scales[0, 4 * quad : 4 * quad + 4, :].bitcast(I32),
            )
        key_rows = keys_words[0].rearrange("p n t -> p (n t)")
        k_words = []
        for h in range(2):
            kw = sb.tile([P, K_PASS], U32, name=f"k_words{h}", align_bytes=64)
            nc.sync.dma_start(out=kw[:].bitcast(I32), in_=key_rows[:, h * 2048 : (h + 1) * 2048].bitcast(I32))
            k_words.append(kw)
        second = lists.tile([P, SLOTS // 16], U16, name="second")
        nc.sync.dma_start(second[:], offs2)
        first = lists.tile([P, SLOTS // 16], U16, name="first")
        nc.sync.dma_start(first[:], offs)
        share_col = sb.tile([P, 1], F32, name="share_col")
        nc.scalar.dma_start(out=share_col[:], in_=share)
        v_raw = []
        for g in range(PASSES):
            vr = sb.tile([P, PACK, E], F32, name=f"v_raw{g}", tag=f"v_raw{g}")
            nc.sync.dma_start(out=vr[:], in_=vals[g * K_PASS : (g + 1) * K_PASS, :].rearrange("(p j) e -> p j e", j=PACK))
            v_raw.append(vr)
        fac_cols = sb.tile([P, PASSES, PACK], F32, name="fac_cols")
        nc.sync.dma_start(out=fac_cols[:], in_=fac[0].rearrange("(g p j) -> p g j", g=PASSES, j=PACK))

        ident = sb.tile([P, P], F32, name="ident")
        make_identity(nc, ident[:])
        df = sb.tile([P, T], F32, name="df")
        nc.vector.memset(df[:], 0.0)

        q_codes = sb.tile([P, Q], U32, name="q_codes", align_bytes=64)
        q_scales = sb.tile([P, Q], U8, name="q_scales", align_bytes=64)
        q_bf = []
        for h in range(2):
            qb = sb.tile([P, 64, PACK], BF16, name=f"q_bf{h}", align_bytes=64)
            nc.vector.tensor_copy(
                out=qb[:].rearrange("p (c i) j -> p c j i", i=4),
                in_=q_raw[:, :, h * 64 : (h + 1) * 64].rearrange("p j (c i) -> p c j i", i=4),
            )
            q_bf.append(qb)
        for h in range(2):
            cols = slice(h * 64, (h + 1) * 64)
            nc.vector.quantize_mx(
                out=q_codes[:, cols].bitcast(FP8X4), scales=q_scales[:, cols], in_=q_bf[h][:].rearrange("p q j -> p (q j)")
            )

        a_sb = sb.tile([P, T], F32, name="a_sb")
        a_ps = []
        for c in range(4):
            cols = slice(c * 256, (c + 1) * 256)
            bank = ps.tile([P, 256], F32, name=f"a_ps{c}", tag=f"bank{c}")
            nc.tensor.matmul_mx(
                out=bank[:],
                lhsT=q_codes[:].bitcast(FP8X4),
                lhsT_scale=q_scales[:],
                rhs=k_words[c // 2][:, (c % 2) * 256 : (c % 2 + 1) * 256].bitcast(FP8X4),
                rhs_scale=k_scales[:, cols],
                start=True,
                stop=True,
            )
            if c % 2 == 1:
                nc.scalar.copy(out=a_sb[:, cols], in_=bank[:])
            else:
                nc.vector.tensor_copy(out=a_sb[:, cols], in_=bank[:])
            a_ps.append(bank)

        share_wide = sb.tile([P, SLOTS], F32, name="share_wide")
        nc.scalar.copy(out=share_wide[:], in_=share_col[:].to_broadcast([P, SLOTS]))

        fac_ps = []
        for g in range(PASSES):
            bank = ps.tile([P, PACK, P], F32, name=f"fac_ps{g}")
            for j in range(PACK):
                nc.tensor.transpose(bank[:, j, :], fac_cols[:, g, j : j + 1].to_broadcast([P, P]), ident[:])
            fac_ps.append(bank)

        own = sb.tile([P, SLOTS], F32, name="own")
        diff = sb.tile([P, SLOTS], F32, name="diff")
        for h in range(2):
            nc.vector.tensor_copy(own[:, h * 256 : (h + 1) * 256], a_sb[:].indirect(first[:, h * 16 : (h + 1) * 16]))
        for h in range(2):
            nc.vector.tensor_tensor(
                diff[:, h * 256 : (h + 1) * 256],
                a_sb[:].indirect(second[:, h * 16 : (h + 1) * 16]),
                own[:, h * 256 : (h + 1) * 256],
                ALU.subtract,
            )
        nc.vector.tensor_tensor(df[:].indirect(first[:]), diff[:], share_wide[:], ALU.mult)

        v_bf = []
        for g in range(PASSES):
            vb = sb.tile([P, E, PACK], BF16, name=f"v_bf{g}", align_bytes=64)
            nc.scalar.copy(
                out=vb[:].rearrange("p (c i) j -> p c j i", i=4),
                in_=v_raw[g][:].rearrange("p j (c i) -> p c j i", i=4),
            )
            v_bf.append(vb)

        s = sb.tile([P, T], F32, name="s", tag="s", align_bytes=64)
        nc.gpsimd.tensor_tensor(s[:, 512:], a_sb[:, 512:], df[:, 512:], ALU.add)
        for c in range(2):
            cols = slice(c * 256, (c + 1) * 256)
            nc.vector.tensor_tensor(s[:, cols], a_ps[c][:], df[:, cols], ALU.add)
        neg_s = sb.tile([P, T], F32, name="neg_s")
        neg_max = sb.tile([P, 1], F32, name="neg_max")
        neg_max_head = sb.tile([P, 1], F32, name="neg_max_head")
        nc.vector.tensor_scalar(neg_s[:, :256], s[:, :256], -1.0, None, ALU.mult, ALU.min, accum_out=neg_max_head[:])
        nc.vector.tensor_scalar(neg_s[:, 256:], s[:, 256:], -1.0, neg_max_head[:], ALU.mult, ALU.min, accum_out=neg_max[:])
        p = sb.tile([P, T], F32, name="p", tag="v_raw1")
        row_sum = sb.tile([P, 1], F32, name="row_sum")
        nc.scalar.activation(p[:], neg_s[:], ACT.Exp, bias=neg_max[:], scale=-1.0, accum_out=row_sum[:])

        v_codes = sb.tile([P, PASSES, E], U32, name="v_codes", tag="s", align_bytes=64)
        v_scales = sb.tile([P, PASSES, E], U8, name="v_scales", align_bytes=64)
        for g in range(PASSES):
            nc.vector.quantize_mx(
                out=v_codes[:, g, :].bitcast(FP8X4), scales=v_scales[:, g, :], in_=v_bf[g][:].rearrange("p e j -> p (e j)")
            )

        inv_sum = sb.tile([P, 1], F32, name="inv_sum")
        nc.vector.reciprocal(inv_sum[:], row_sum[:])

        o_ps = [ps.tile([P, E_HALF], F32, name=f"o_ps{c}", tag=f"bank{c}") for c in range(4)]
        turned_banks = []
        for g in range(PASSES):
            p_pass = p[:, g * K_PASS : (g + 1) * K_PASS].rearrange("q (r j) -> q r j", j=PACK)
            fac_pass = fac_ps[g][:].rearrange("q j r -> q r j")
            turned = ps.tile([P, 2, Q], F32, name=f"turned{g}", tag=f"bank{4 + g}")
            for u in range(2):
                wb = sb.tile([P, P, 2], BF16, name=f"w_bf{g}{u}")
                nc.vector.scalar_tensor_tensor(
                    wb[:], p_pass[:, :, 2 * u : 2 * u + 2], inv_sum[:], fac_pass[:, :, 2 * u : 2 * u + 2], ALU.mult, ALU.mult
                )
                nc.tensor.transpose(turned[:, u, :], wb[:].rearrange("q r e -> q (r e)").bitcast(F32), ident[:])
            turned_banks.append(turned)
        for g in range(PASSES):
            turned = turned_banks[g]
            wt_bf = sb.tile([P, Q * PACK], BF16, name=f"wt_bf{g}", align_bytes=64)
            nc.scalar.copy(
                out=wt_bf[:].bitcast(F32).rearrange("r (q u) -> r q u", u=2), in_=turned[:].rearrange("r u q -> r q u")
            )
            wt_codes = sb.tile([P, Q], U32, name=f"wt_codes{g}", align_bytes=64)
            wt_scales = sb.tile([P, Q], U8, name=f"wt_scales{g}", align_bytes=64)
            nc.vector.quantize_mx(out=wt_codes[:].bitcast(FP8X4), scales=wt_scales[:], in_=wt_bf[:])
            for c in range(4):
                cols = slice(c * E_HALF, (c + 1) * E_HALF)
                nc.tensor.matmul_mx(
                    out=o_ps[c][:],
                    lhsT=wt_codes[:].bitcast(FP8X4),
                    lhsT_scale=wt_scales[:],
                    rhs=v_codes[:, g, cols].bitcast(FP8X4),
                    rhs_scale=v_scales[:, g, cols],
                    start=(g == 0),
                    stop=(g == PASSES - 1),
                )
        for c in range(4):
            cols = slice(c * E_HALF, (c + 1) * E_HALF)
            res = sb.tile([P, E_HALF], F32, name=f"res{c}")
            if c % 2 == 0:
                nc.scalar.copy(out=res[:], in_=o_ps[c][:])
            else:
                nc.vector.tensor_copy(out=res[:], in_=o_ps[c][:])
            nc.sync.dma_start(out=out[:, cols], in_=res[:])
